import numpy as np
import ml_dtypes


def mxq(x, axis, fmt="e4m3"):
    dtype, down = {"e4m3": (ml_dtypes.float8_e4m3fn, 7), "e5m2": (ml_dtypes.float8_e5m2, 14)}[fmt]
    v = np.moveaxis(np.asarray(x, np.float32).astype(ml_dtypes.bfloat16).astype(np.float64), axis, -1)
    blocks = v.reshape(v.shape[:-1] + (-1, 32))
    amax = np.abs(blocks).max(-1, keepdims=True)
    byte = np.maximum(np.where(amax > 0, np.frexp(amax)[1] - 1 + 127, 0) - down, 1)
    scale = np.exp2(byte - 127.0)
    codes = (blocks / scale).astype(np.float32).astype(dtype).astype(np.float64)
    return np.moveaxis((codes * scale).reshape(v.shape), -1, axis)


WIDE = False


def mx_kscale(k):
    if not WIDE:
        return np.ones(k)
    levels = np.array([10, -10, 5, -5, 0])
    if k % 512:
        return np.exp2(np.random.permutation(np.resize(levels, k // 32))).repeat(32)
    a = np.empty((k // 512, 16))
    for p in range(k // 512):
        a[p, :8] = np.random.permutation(np.resize(levels, 8))
        for g in range(8):
            far = levels[np.abs(levels - a[p, g]) >= 10]
            a[p, g + 8] = far[np.random.randint(len(far))]
    return np.exp2(a.ravel()).repeat(32)


def f64(x):
    return np.asarray(x).astype(np.float64)


def striped(idx):
    return np.tile(idx.reshape(-1, 16).T, (8, 1)).astype(np.uint16)


def unstriped(offs):
    return offs[:16].T.reshape(-1).astype(np.int64)


def pack_weight(w):
    k, n = w.shape
    w = f64(np.asarray(w, np.float32).astype(ml_dtypes.bfloat16)).reshape(k // 32, 32, n)
    amax = np.abs(w).max(1)
    byte = np.clip(np.where(amax > 0, np.frexp(amax)[1] - 1 + 127 - 7, 1), 1, 254)
    scaled = (w * np.exp2(127.0 - byte)[:, None, :]).reshape(k, n).astype(np.float32)
    words = np.ascontiguousarray(scaled.reshape(k // 512, 128, 4, n).transpose(0, 1, 3, 2)).astype(ml_dtypes.float8_e4m3fn).view(np.uint8)
    return words, np.ascontiguousarray(byte.astype(np.uint8).reshape(k // 512, 16, n))


def unpack_weight(words, scales):
    g, p, n, _ = words.shape
    vals = np.ascontiguousarray(words).view(ml_dtypes.float8_e4m3fn).astype(np.float64) * np.repeat(np.exp2(scales.astype(np.float64) - 127.0), 8, axis=1)[..., None]
    return vals.transpose(0, 1, 3, 2).reshape(g * 512, n)


H, K, T, S, N = 512, 512, 2048, 1024, 256


def setup_inputs():
    n = np.random.standard_normal
    s = mx_kscale(K)[:, None]
    u = mx_kscale(H)
    packed_xT = pack_weight(n((K, T)) * s)
    return {
        "x_words": packed_xT[0],
        "x_scales": packed_xT[1],
        "w1": (n((K, H)) / np.sqrt(K) / s).astype(np.float32),
        "unit": (np.random.uniform(0.5, 1.5, (H, 1)) * u[:, None]).astype(np.float32),
        "wo": (n((H, N)) / np.sqrt(H) / u[:, None]).astype(np.float32),
        "skip": (n((N, S))).astype(np.float32),
        "offs": striped(np.random.permutation(T)[:S]),
    }


def reference(x_words, x_scales, w1, unit, wo, skip, offs):
    xq = unpack_weight(x_words, x_scales)[:, unstriped(offs)]
    y = mxq(f64(w1), 0, "e4m3").T @ xq
    lum = np.exp(y)
    lmean = y.mean(axis=1, keepdims=True)
    key = np.exp(lmean)
    sc = 0.8 * (lum / key)
    tm = sc / (np.maximum(np.maximum(np.pad(sc, ((0, 0), (1, 0)))[:, :S], sc), np.pad(sc, ((0, 0), (0, 1)))[:, 1:]) + 1.0)
    zz = f64(unit) * tm
    return (mxq(f64(wo), 0, "e4m3").T @ mxq(zz, 0, "e4m3")) + f64(skip)

@@ -1,0 +1,237 @@
+import math
+from contextlib import ExitStack
+
+import concourse.mybir as mybir
+
+H, K, T, S, N = 512, 512, 2048, 1024, 256
+FLOPS = 2 * K * H * S + 2 * H * N * S
+
+F32 = mybir.dt.float32
+BF16 = mybir.dt.bfloat16
+I32 = mybir.dt.int32
+U32 = mybir.dt.uint32
+U16 = mybir.dt.uint16
+U8 = mybir.dt.uint8
+FP8X4 = mybir.dt.float8_e4m3fn_x4
+ALU = mybir.AluOpType
+ACT = mybir.ActivationFunctionType
+
+P = 128
+PACK = 4
+BANK = 512
+PAIRS = S // 2
+PAD = 8
+LOWEST = -(2.0**127)
+LN_EDGE = 2.0**63
+CHUNKS = (64, 128, 128, 128, 64)
+
+
+def tile_picked_ytonem_local_p_kernel(tc, x_words, x_scales, w1, unit, wo, skip, offs, out):
+    nc = tc.nc
+    with ExitStack() as ctx:
+        keep = ctx.enter_context(tc.tile_pool(name="keep", bufs=1))
+        psum = ctx.enter_context(tc.psum_pool(name="psum", bufs=1))
+
+        offsets = keep.tile([P, S // 16], U16, name="offsets")
+        nc.sync.dma_start(offsets[:], offs)
+        unit_sb = keep.tile([P, PACK], F32, name="unit_sb")
+        nc.sync.dma_start(unit_sb[:], unit.rearrange("(p t) o -> p (t o)", t=PACK))
+
+        table_scales = keep.tile([P, T], U8, name="table_scales", align_bytes=64)
+        nc.vector.memset(table_scales[:].bitcast(I32), 0)
+        for q in range(4):
+            nc.scalar.dma_start(
+                table_scales[32 * q : 32 * q + 4, :].bitcast(I32), x_scales[0, 4 * q : 4 * q + 4, :].bitcast(I32)
+            )
+        table_words = keep.tile([P, T], I32, name="table_words", tag="table", align_bytes=64)
+        words_hbm = x_words[0].rearrange("p n t -> p (n t)").bitcast(I32)
+        for half in range(2):
+            cols = slice(half * T // 2, (half + 1) * T // 2)
+            nc.sync.dma_start(table_words[:, cols], words_hbm[:, cols])
+        w1_rows = w1.rearrange("(p j) c -> p j c", j=PACK)
+        w1_raw = []
+        for half in range(2):
+            raw = keep.tile([P, PACK, H // 2], F32, name=f"w1_raw{half}", tag=f"weights{half}")
+            nc.sync.dma_start(raw[:], w1_rows[:, :, half * H // 2 : (half + 1) * H // 2])
+            w1_raw.append(raw)
+        magnitude = keep.tile([P, PACK], F32, name="magnitude")
+        nc.vector.scalar_tensor_tensor(magnitude[:], unit_sb[:], -1.0, unit_sb[:], ALU.mult, ALU.max)
+        factors = keep.tile([P, 3, PACK], F32, name="factors")
+        nc.vector.tensor_scalar(factors[:, 0, :], magnitude[:], 1.0 / LN_EDGE, LN_EDGE, ALU.max, ALU.min)
+        nc.vector.tensor_scalar(factors[:, 1, :], magnitude[:], LN_EDGE, 1.0 / LN_EDGE, ALU.max, ALU.mult)
+        nc.vector.tensor_scalar(factors[:, 2, :], magnitude[:], 1.0 / LN_EDGE, LN_EDGE, ALU.min, ALU.mult)
+        logs = keep.tile([P, 3, PACK], F32, name="logs")
+        nc.scalar.activation(logs[:, 0:2, :], factors[:, 0:2, :], ACT.Ln)
+        nc.scalar.activation(logs[:, 2, :], factors[:, 2, :], ACT.Ln, bias=0.5 / LN_EDGE, scale=0.8)
+        log_gain = keep.tile([P, PACK], F32, name="log_gain")
+        nc.vector.tensor_reduce(log_gain[:], logs[:].rearrange("p f t -> p t f"), mybir.AxisListType.X, ALU.add)
+        warm = keep.tile([P, 1], F32, name="warm")
+        nc.scalar.activation(warm[:], logs[:, 2, 0:1], ACT.Exp)
+        twice = keep.tile([P, PACK], F32, name="twice")
+        nc.gpsimd.tensor_scalar(twice[:], unit_sb[:], 0.0, 2.0, ALU.is_ge, ALU.mult)
+        unit_sign = keep.tile([P, PACK], F32, name="unit_sign")
+        nc.gpsimd.tensor_scalar(unit_sign[:], twice[:], -1.0, 1.0, ALU.add, ALU.mult)
+
+        y_sb = []
+        for t in range(PACK):
+            y_t = keep.tile([P, 2, PAIRS + PAD], F32, name=f"y{t}", tag=f"row{t}")
+            nc.gpsimd.memset(y_t[:, 0, PAIRS:], LOWEST)
+            y_sb.append(y_t)
+
+        def gather(half):
+            entries = offsets[:, half * BANK // 16 : (half + 1) * BANK // 16]
+            scales = keep.tile([P, BANK], U8, name=f"picked_scales{half}", align_bytes=64)
+            nc.vector.tensor_copy(scales[:], table_scales[:].indirect(entries))
+            words = keep.tile([P, BANK], U32, name=f"picked_words{half}", align_bytes=64)
+            nc.vector.tensor_copy(words[:], table_words[:].bitcast(U32).indirect(entries))
+            return words, scales
+
+        picked = [gather(0)]
+
+        w1_bf = keep.tile([P, PACK, P, PACK], BF16, name="w1_bf", align_bytes=64)
+        w1_dealt = w1_bf[:].rearrange("p t m j -> p m t j")
+
+        def w1_source(half):
+            return w1_raw[half][:].rearrange("p j (m t) -> p m t j", t=PACK)
+
+        nc.scalar.copy(w1_dealt[:, 0:64], w1_source(0))
+        nc.scalar.copy(w1_dealt[:, 64:88], w1_source(1)[:, 0:24])
+        nc.vector.tensor_copy(w1_dealt[:, 88:128], w1_source(1)[:, 24:64])
+        w1_codes = keep.tile([P, H], U32, name="w1_codes", align_bytes=64)
+        w1_scales = keep.tile([P, H], U8, name="w1_scales", align_bytes=64)
+        for t in range(PACK):
+            cols = slice(t * P, (t + 1) * P)
+            nc.vector.quantize_mx(
+                out=w1_codes[:, cols].bitcast(FP8X4),
+                scales=w1_scales[:, cols],
+                in_=w1_bf[:, t].rearrange("p m j -> p (m j)"),
+            )
+
+        sums = keep.tile([P, 2, PACK], F32, name="sums")
+        half_bias = keep.tile([P, PACK], F32, name="half_bias")
+        exp_bias = keep.tile([P, PACK], F32, name="exp_bias")
+        picked.append(gather(1))
+        for half in range(2):
+            if True:
+                for t in range(PACK):
+                    cols = slice(t * P, (t + 1) * P)
+                    bank = psum.tile([P, BANK], F32, name=f"y_bank{t}{half}", tag=f"bank{2 * t + half}")
+                    nc.tensor.matmul_mx(
+                        out=bank[:],
+                        lhsT=w1_codes[:, cols].bitcast(FP8X4),
+                        lhsT_scale=w1_scales[:, cols],
+                        rhs=picked[half][0][:].bitcast(FP8X4),
+                        rhs_scale=picked[half][1][:],
+                        start=True,
+                        stop=True,
+                    )
+                    planes = y_sb[t][:, :, half * BANK // 2 : (half + 1) * BANK // 2]
+                    by_parity = bank[:].rearrange("p (k two) -> p two k", two=2)
+                    total = sums[:, half, t : t + 1]
+                    if half == 0 or t % 2 == 0:
+                        nc.scalar.activation(planes, by_parity, ACT.Copy, accum_out=total)
+                    else:
+                        nc.vector.tensor_scalar(planes, by_parity, 1.0, None, ALU.mult, ALU.add, accum_out=total)
+                    before, after = (log_gain, half_bias) if half == 0 else (half_bias, exp_bias)
+                    nc.gpsimd.tensor_scalar(
+                        after[:, t : t + 1], total, -1.0 / S, before[:, t : t + 1], ALU.mult, ALU.add
+                    )
+        wo_raw = keep.tile([P, PACK, N], F32, name="wo_raw", tag="weights0")
+        nc.sync.dma_start(wo_raw[:], wo.rearrange("(p j) n -> p j n", j=PACK))
+        skip_sb = keep.tile([P, 2, S], F32, name="skip_sb", tag="table", align_bytes=64)
+        for mt in range(2):
+            nc.sync.dma_start(skip_sb[:, mt, :], skip[mt * P : (mt + 1) * P, :])
+
+        whole_sums = keep.tile([P, PACK], F32, name="whole_sums")
+        nc.gpsimd.tensor_tensor(whole_sums[:], sums[:, 0, :], sums[:, 1, :], ALU.add)
+        sigmoid_bias = keep.tile([P, PACK], F32, name="sigmoid_bias")
+        nc.gpsimd.tensor_scalar(sigmoid_bias[:], whole_sums[:], 1.0 / S, -math.log(0.8), ALU.mult, ALU.add)
+
+        numerator = keep.tile([P, PACK, 2, PAIRS], F32, name="numerator")
+        for t in range(PACK):
+            nc.scalar.activation(numerator[:, t], y_sb[t][:, :, 0:PAIRS], ACT.Exp, bias=exp_bias[:, t : t + 1])
+
+        pair_max = []
+        for t in range(PACK):
+            pair_t = keep.tile([P, PAIRS], F32, name=f"pair_max{t}")
+            pair_max.append(pair_t)
+        largest = []
+        for t in range(PACK):
+            largest_t = keep.tile([P, 2, PAIRS], F32, name=f"largest{t}")
+            largest.append(largest_t)
+
+        def pair_step(t):
+            nc.vector.tensor_tensor(pair_max[t][:], y_sb[t][:, 0, 0:PAIRS], y_sb[t][:, 1, 0:PAIRS], ALU.max)
+
+        def neighbour_step(t):
+            flat = y_sb[t][:].rearrange("p two k -> p (two k)")
+            odd_before = flat[:, PAIRS + PAD - 1 : 2 * PAIRS + PAD - 1]
+            even_after = flat[:, 1 : PAIRS + 1]
+            nc.vector.tensor_tensor(largest[t][:, 0, :], pair_max[t][:], odd_before, ALU.max)
+            nc.vector.tensor_tensor(largest[t][:, 1, :], pair_max[t][:], even_after, ALU.max)
+
+        pair_step(0)
+        for t in range(PACK):
+            if t + 1 < PACK:
+                pair_step(t + 1)
+            neighbour_step(t)
+
+        out_rows = out.rearrange("(mt p) n -> p mt n", p=P)
+        first = 0
+        for c, pairs in enumerate(CHUNKS):
+            ks = slice(first, first + pairs)
+            entries = slice(2 * first, 2 * (first + pairs))
+            width = 2 * pairs
+            first = first + pairs
+            damping = keep.tile([P, PACK, 2, pairs], F32, name=f"damping{c}", tag=f"row{PACK - 1 - c}" if c < PACK else f"damping{c}")
+            for t in range(PACK):
+                nc.scalar.activation(
+                    damping[:, t], largest[t][:, :, ks], ACT.Sigmoid, bias=sigmoid_bias[:, t : t + 1], scale=-1.0
+                )
+            zz_bf = keep.tile([P, 2, pairs, PACK], BF16, name=f"zz_bf{c}", align_bytes=64)
+            for parity in range(2):
+                nc.vector.tensor_tensor(
+                    zz_bf[:, parity].rearrange("p (c i) t -> p c t i", i=4),
+                    numerator[:, :, parity, ks].rearrange("p t (c i) -> p c t i", i=4),
+                    damping[:, :, parity, :].rearrange("p t (c i) -> p c t i", i=4),
+                    ALU.mult,
+                )
+            zz_codes = keep.tile([P, width], U32, name=f"zz_codes{c}", align_bytes=64)
+            zz_scales = keep.tile([P, width], U8, name=f"zz_scales{c}", align_bytes=64)
+            nc.vector.quantize_mx(
+                out=zz_codes[:].bitcast(FP8X4), scales=zz_scales[:], in_=zz_bf[:].rearrange("p two k t -> p (two k t)")
+            )
+            if c == 0:
+                wo_planes = keep.tile([P, PACK, N], BF16, name="wo_planes")
+                for j in range(PACK):
+                    nc.scalar.activation(wo_planes[:, j, :], wo_raw[:, j, :], ACT.Copy, scale=unit_sign[:, j : j + 1])
+                wo_bf = keep.tile([P, N, PACK], BF16, name="wo_bf", align_bytes=64)
+                nc.scalar.copy(
+                    wo_bf[:].rearrange("p (c i) j -> p c j i", i=4),
+                    wo_planes[:].rearrange("p j (c i) -> p c j i", i=4),
+                )
+                wo_codes = keep.tile([P, N], U32, name="wo_codes", align_bytes=64)
+                wo_scales = keep.tile([P, N], U8, name="wo_scales", align_bytes=64)
+                nc.vector.quantize_mx(
+                    out=wo_codes[:].bitcast(FP8X4), scales=wo_scales[:], in_=wo_bf[:].rearrange("p n j -> p (n j)")
+                )
+            readout = psum.tile([P, 2, width], F32, name=f"readout{c}", tag=f"bank{c}")
+            for mt in range(2):
+                cols = slice(mt * P, (mt + 1) * P)
+                nc.tensor.matmul_mx(
+                    out=readout[:, mt, :],
+                    lhsT=wo_codes[:, cols].bitcast(FP8X4),
+                    lhsT_scale=wo_scales[:, cols],
+                    rhs=zz_codes[:].bitcast(FP8X4),
+                    rhs_scale=zz_scales[:],
+                    start=True,
+                    stop=True,
+                )
+            result = keep.tile([P, 2, width], F32, name=f"result{c}")
+            nc.vector.tensor_tensor(
+                result[:].rearrange("p mt (k two) -> p mt k two", two=2),
+                readout[:].rearrange("p mt (two k) -> p mt k two", two=2),
+                skip_sb[:, :, entries].rearrange("p mt (k two) -> p mt k two", two=2),
+                ALU.add,
+            )
+            nc.sync.dma_start(out_rows[:, :, entries], result[:])

@@ -21,8 +21,9 @@ PACK = 4
 BANK = 512
 PAIRS = S // 2
 PAD = 8
-LOWEST = -(2.0**127)
+HIGHEST = 2.0**127
 LN_EDGE = 2.0**63
+VECTOR_TILES = (1, 3)
 CHUNKS = (64, 128, 128, 128, 64)
 
 
@@ -75,28 +76,33 @@ def tile_picked_ytonem_local_p_kernel(tc, x_words, x_scales, w1, unit, wo, skip,
         y_sb = []
         for t in range(PACK):
             y_t = keep.tile([P, 2, PAIRS + PAD], F32, name=f"y{t}", tag=f"row{t}")
-            nc.gpsimd.memset(y_t[:, 0, PAIRS:], LOWEST)
+            nc.gpsimd.memset(y_t[:, 0, PAIRS:], HIGHEST)
             y_sb.append(y_t)
 
         def gather(half):
             entries = offsets[:, half * BANK // 16 : (half + 1) * BANK // 16]
-            scales = keep.tile([P, BANK], U8, name=f"picked_scales{half}", align_bytes=64)
+            scales = keep.tile([P, BANK], U8, name=f"picked_scales{half}", tag=f"scales_slot{half}", align_bytes=64)
             nc.vector.tensor_copy(scales[:], table_scales[:].indirect(entries))
-            words = keep.tile([P, BANK], U32, name=f"picked_words{half}", align_bytes=64)
+            words = keep.tile([P, BANK], U32, name=f"picked_words{half}", tag=f"words_slot{half}", align_bytes=64)
             nc.vector.tensor_copy(words[:], table_words[:].bitcast(U32).indirect(entries))
             return words, scales
 
         picked = [gather(0)]
 
-        w1_bf = keep.tile([P, PACK, P, PACK], BF16, name="w1_bf", align_bytes=64)
-        w1_dealt = w1_bf[:].rearrange("p t m j -> p m t j")
-
-        def w1_source(half):
-            return w1_raw[half][:].rearrange("p j (m t) -> p m t j", t=PACK)
-
-        nc.scalar.copy(w1_dealt[:, 0:64], w1_source(0))
-        nc.scalar.copy(w1_dealt[:, 64:88], w1_source(1)[:, 0:24])
-        nc.vector.tensor_copy(w1_dealt[:, 88:128], w1_source(1)[:, 24:64])
+        w1_bf = [
+            keep.tile([P, 2, P, PACK], BF16, name="w1_bf_low", tag="scales_slot1", align_bytes=64),
+            keep.tile([P, 2, P, PACK], BF16, name="w1_bf_high", tag="words_slot1", align_bytes=64),
+        ]
+        for pair in range(2):
+            dealt = w1_bf[pair][:].rearrange("p t m j -> p m t j")
+            ts = slice(2 * pair, 2 * pair + 2)
+            low = w1_raw[0][:].rearrange("p j (m t) -> p m t j", t=PACK)[:, :, ts]
+            high = w1_raw[1][:].rearrange("p j (m t) -> p m t j", t=PACK)[:, :, ts]
+            nc.scalar.copy(dealt[:, 0:64], low)
+            if pair == 0:
+                nc.vector.tensor_copy(dealt[:, 64:128], high)
+            else:
+                nc.scalar.copy(dealt[:, 64:128], high)
         w1_codes = keep.tile([P, H], U32, name="w1_codes", align_bytes=64)
         w1_scales = keep.tile([P, H], U8, name="w1_scales", align_bytes=64)
         for t in range(PACK):
@@ -104,10 +110,11 @@ def tile_picked_ytonem_local_p_kernel(tc, x_words, x_scales, w1, unit, wo, skip,
             nc.vector.quantize_mx(
                 out=w1_codes[:, cols].bitcast(FP8X4),
                 scales=w1_scales[:, cols],
-                in_=w1_bf[:, t].rearrange("p m j -> p (m j)"),
+                in_=w1_bf[t // 2][:, t % 2].rearrange("p m j -> p (m j)"),
             )
 
-        sums = keep.tile([P, 2, PACK], F32, name="sums")
+        first_sums = keep.tile([P, PACK], F32, name="first_sums")
+        second_sums = keep.tile([P, PACK], F32, name="second_sums")
         half_bias = keep.tile([P, PACK], F32, name="half_bias")
         exp_bias = keep.tile([P, PACK], F32, name="exp_bias")
         picked.append(gather(1))
@@ -127,29 +134,31 @@ def tile_picked_ytonem_local_p_kernel(tc, x_words, x_scales, w1, unit, wo, skip,
                     )
                     planes = y_sb[t][:, :, half * BANK // 2 : (half + 1) * BANK // 2]
                     by_parity = bank[:].rearrange("p (k two) -> p two k", two=2)
-                    total = sums[:, half, t : t + 1]
-                    if half == 0 or t % 2 == 0:
-                        nc.scalar.activation(planes, by_parity, ACT.Copy, accum_out=total)
+                    if half == 0:
+                        nc.scalar.activation(planes, by_parity, ACT.Copy, scale=-1.0 / S, accum_out=first_sums[:, t : t + 1])
+                    elif t in VECTOR_TILES:
+                        nc.vector.tensor_scalar(
+                            planes, by_parity, -1.0 / S, half_bias[:, t : t + 1], ALU.mult, ALU.add, accum_out=exp_bias[:, t : t + 1]
+                        )
                     else:
-                        nc.vector.tensor_scalar(planes, by_parity, 1.0, None, ALU.mult, ALU.add, accum_out=total)
-                    before, after = (log_gain, half_bias) if half == 0 else (half_bias, exp_bias)
-                    nc.gpsimd.tensor_scalar(
-                        after[:, t : t + 1], total, -1.0 / S, before[:, t : t + 1], ALU.mult, ALU.add
-                    )
+                        nc.scalar.activation(planes, by_parity, ACT.Copy, scale=-1.0 / S, accum_out=second_sums[:, t : t + 1])
+                        nc.scalar.activation(
+                            exp_bias[:, t : t + 1], second_sums[:, t : t + 1], ACT.Identity, bias=half_bias[:, t : t + 1]
+                        )
+            if half == 0:
+                nc.vector.tensor_tensor(half_bias[:], first_sums[:], log_gain[:], ALU.add)
         wo_raw = keep.tile([P, PACK, N], F32, name="wo_raw", tag="weights0")
         nc.sync.dma_start(wo_raw[:], wo.rearrange("(p j) n -> p j n", j=PACK))
         skip_sb = keep.tile([P, 2, S], F32, name="skip_sb", tag="table", align_bytes=64)
         for mt in range(2):
             nc.sync.dma_start(skip_sb[:, mt, :], skip[mt * P : (mt + 1) * P, :])
 
-        whole_sums = keep.tile([P, PACK], F32, name="whole_sums")
-        nc.gpsimd.tensor_tensor(whole_sums[:], sums[:, 0, :], sums[:, 1, :], ALU.add)
         sigmoid_bias = keep.tile([P, PACK], F32, name="sigmoid_bias")
-        nc.gpsimd.tensor_scalar(sigmoid_bias[:], whole_sums[:], 1.0 / S, -math.log(0.8), ALU.mult, ALU.add)
+        nc.vector.scalar_tensor_tensor(sigmoid_bias[:], log_gain[:], -math.log(0.8), exp_bias[:], ALU.add, ALU.subtract)
 
         numerator = keep.tile([P, PACK, 2, PAIRS], F32, name="numerator")
         for t in range(PACK):
-            nc.scalar.activation(numerator[:, t], y_sb[t][:, :, 0:PAIRS], ACT.Exp, bias=exp_bias[:, t : t + 1])
+            nc.scalar.activation(numerator[:, t], y_sb[t][:, :, 0:PAIRS], ACT.Exp, bias=exp_bias[:, t : t + 1], scale=-float(S))
 
         pair_max = []
         for t in range(PACK):
@@ -161,14 +170,15 @@ def tile_picked_ytonem_local_p_kernel(tc, x_words, x_scales, w1, unit, wo, skip,
             largest.append(largest_t)
 
         def pair_step(t):
-            nc.vector.tensor_tensor(pair_max[t][:], y_sb[t][:, 0, 0:PAIRS], y_sb[t][:, 1, 0:PAIRS], ALU.max)
+            nc.vector.tensor_tensor(pair_max[t][:], y_sb[t][:, 0, 0:PAIRS], y_sb[t][:, 1, 0:PAIRS], ALU.min)
 
         def neighbour_step(t):
             flat = y_sb[t][:].rearrange("p two k -> p (two k)")
-            odd_before = flat[:, PAIRS + PAD - 1 : 2 * PAIRS + PAD - 1]
-            even_after = flat[:, 1 : PAIRS + 1]
-            nc.vector.tensor_tensor(largest[t][:, 0, :], pair_max[t][:], odd_before, ALU.max)
-            nc.vector.tensor_tensor(largest[t][:, 1, :], pair_max[t][:], even_after, ALU.max)
+            reach = PAIRS + PAD - 2
+            outer = flat[:, 1 : 1 + 2 * reach].rearrange("p (two k) -> p two k", two=2)[:, :, 0:PAIRS]
+            nc.vector.tensor_tensor(
+                largest[t][:], pair_max[t][:].unsqueeze(1).to_broadcast([P, 2, PAIRS]), outer, ALU.min
+            )
 
         pair_step(0)
         for t in range(PACK):
@@ -186,14 +196,14 @@ def tile_picked_ytonem_local_p_kernel(tc, x_words, x_scales, w1, unit, wo, skip,
             damping = keep.tile([P, PACK, 2, pairs], F32, name=f"damping{c}", tag=f"row{PACK - 1 - c}" if c < PACK else f"damping{c}")
             for t in range(PACK):
                 nc.scalar.activation(
-                    damping[:, t], largest[t][:, :, ks], ACT.Sigmoid, bias=sigmoid_bias[:, t : t + 1], scale=-1.0
+                    damping[:, t], largest[t][:, :, ks], ACT.Sigmoid, bias=sigmoid_bias[:, t : t + 1], scale=float(S)
                 )
             zz_bf = keep.tile([P, 2, pairs, PACK], BF16, name=f"zz_bf{c}", align_bytes=64)
             for parity in range(2):
                 nc.vector.tensor_tensor(
-                    zz_bf[:, parity].rearrange("p (c i) t -> p c t i", i=4),
-                    numerator[:, :, parity, ks].rearrange("p t (c i) -> p c t i", i=4),
-                    damping[:, :, parity, :].rearrange("p t (c i) -> p c t i", i=4),
+                    zz_bf[:, parity].rearrange("p (c i) t -> p c t i", i=2),
+                    numerator[:, :, parity, ks].rearrange("p t (c i) -> p c t i", i=2),
+                    damping[:, :, 1 - parity, :].rearrange("p t (c i) -> p c t i", i=2),
                     ALU.mult,
                 )
             zz_codes = keep.tile([P, width], U32, name=f"zz_codes{c}", align_bytes=64)
@@ -202,13 +212,12 @@ def tile_picked_ytonem_local_p_kernel(tc, x_words, x_scales, w1, unit, wo, skip,
                 out=zz_codes[:].bitcast(FP8X4), scales=zz_scales[:], in_=zz_bf[:].rearrange("p two k t -> p (two k t)")
             )
             if c == 0:
-                wo_planes = keep.tile([P, PACK, N], BF16, name="wo_planes")
-                for j in range(PACK):
-                    nc.scalar.activation(wo_planes[:, j, :], wo_raw[:, j, :], ACT.Copy, scale=unit_sign[:, j : j + 1])
                 wo_bf = keep.tile([P, N, PACK], BF16, name="wo_bf", align_bytes=64)
-                nc.scalar.copy(
-                    wo_bf[:].rearrange("p (c i) j -> p c j i", i=4),
-                    wo_planes[:].rearrange("p j (c i) -> p c j i", i=4),
+                nc.vector.tensor_tensor(
+                    wo_bf[:].rearrange("p (c i) j -> p c j i", i=2),
+                    wo_raw[:].rearrange("p j (c i) -> p c j i", i=2),
+                    unit_sign[:].unsqueeze(1).unsqueeze(3).to_broadcast([P, N // 2, PACK, 2]),
+                    ALU.mult,
                 )
                 wo_codes = keep.tile([P, N], U32, name="wo_codes", align_bytes=64)
                 wo_scales = keep.tile([P, N], U8, name="wo_scales", align_bytes=64)

@@ -21,13 +21,16 @@ PACK = 4
 BANK = 512
 PAIRS = S // 2
 PAD = 8
-HIGHEST = 2.0**127
+PAD_EXPONENT = 88.0
 LN_EDGE = 2.0**63
-VECTOR_TILES = (1, 3)
-CHUNKS = (64, 128, 128, 128, 64)
+SEAM = PAIRS // 2 - 4
+FIRST_VECTOR_TILE = 2
+CHUNKS = (32, 64, 128, 128, 128, 32)
 
 
-def tile_picked_ytonem_local_p_kernel(tc, x_words, x_scales, w1, unit, wo, skip, offs, out):
+def tile_picked_ytonem_local_p_kernel(
+    tc, x_words, x_scales, w1, unit, wo, skip, offs, out
+):
     nc = tc.nc
     with ExitStack() as ctx:
         keep = ctx.enter_context(tc.tile_pool(name="keep", bufs=1))
@@ -38,23 +41,22 @@ def tile_picked_ytonem_local_p_kernel(tc, x_words, x_scales, w1, unit, wo, skip,
         unit_sb = keep.tile([P, PACK], F32, name="unit_sb")
         nc.sync.dma_start(unit_sb[:], unit.rearrange("(p t) o -> p (t o)", t=PACK))
 
+        w1_rows = w1.rearrange("(p j) c -> p j c", j=PACK)
+        w1_early = keep.tile([P, PACK, H // 2], F32, name="w1_early")
+        nc.sync.dma_start(w1_early[:], w1_rows[:, :, 0 : H // 2])
         table_scales = keep.tile([P, T], U8, name="table_scales", align_bytes=64)
         nc.vector.memset(table_scales[:].bitcast(I32), 0)
         for q in range(4):
-            nc.scalar.dma_start(
+            nc.sync.dma_start(
                 table_scales[32 * q : 32 * q + 4, :].bitcast(I32), x_scales[0, 4 * q : 4 * q + 4, :].bitcast(I32)
             )
+        w1_late = keep.tile([P, PACK, H // 2], F32, name="w1_late", tag="w1_late")
+        nc.sync.dma_start(w1_late[:], w1_rows[:, :, H // 2 : H])
         table_words = keep.tile([P, T], I32, name="table_words", tag="table", align_bytes=64)
-        words_hbm = x_words[0].rearrange("p n t -> p (n t)").bitcast(I32)
-        for half in range(2):
-            cols = slice(half * T // 2, (half + 1) * T // 2)
-            nc.sync.dma_start(table_words[:, cols], words_hbm[:, cols])
-        w1_rows = w1.rearrange("(p j) c -> p j c", j=PACK)
-        w1_raw = []
-        for half in range(2):
-            raw = keep.tile([P, PACK, H // 2], F32, name=f"w1_raw{half}", tag=f"weights{half}")
-            nc.sync.dma_start(raw[:], w1_rows[:, :, half * H // 2 : (half + 1) * H // 2])
-            w1_raw.append(raw)
+        nc.sync.dma_start(table_words[:], x_words[0].rearrange("p n t -> p (n t)").bitcast(I32))
+        wo_raw = keep.tile([P, PACK, N], F32, name="wo_raw")
+        nc.sync.dma_start(wo_raw[:], wo.rearrange("(p j) n -> p j n", j=PACK))
+
         magnitude = keep.tile([P, PACK], F32, name="magnitude")
         nc.vector.scalar_tensor_tensor(magnitude[:], unit_sb[:], -1.0, unit_sb[:], ALU.mult, ALU.max)
         factors = keep.tile([P, 3, PACK], F32, name="factors")
@@ -66,43 +68,26 @@ def tile_picked_ytonem_local_p_kernel(tc, x_words, x_scales, w1, unit, wo, skip,
         nc.scalar.activation(logs[:, 2, :], factors[:, 2, :], ACT.Ln, bias=0.5 / LN_EDGE, scale=0.8)
         log_gain = keep.tile([P, PACK], F32, name="log_gain")
         nc.vector.tensor_reduce(log_gain[:], logs[:].rearrange("p f t -> p t f"), mybir.AxisListType.X, ALU.add)
-        warm = keep.tile([P, 1], F32, name="warm")
-        nc.scalar.activation(warm[:], logs[:, 2, 0:1], ACT.Exp)
-        twice = keep.tile([P, PACK], F32, name="twice")
-        nc.gpsimd.tensor_scalar(twice[:], unit_sb[:], 0.0, 2.0, ALU.is_ge, ALU.mult)
+        twice_positive = keep.tile([P, PACK], F32, name="twice_positive")
+        nc.gpsimd.tensor_scalar(twice_positive[:], unit_sb[:], 0.0, 2.0, ALU.is_ge, ALU.mult)
         unit_sign = keep.tile([P, PACK], F32, name="unit_sign")
-        nc.gpsimd.tensor_scalar(unit_sign[:], twice[:], -1.0, 1.0, ALU.add, ALU.mult)
+        nc.gpsimd.tensor_scalar(unit_sign[:], twice_positive[:], -1.0, 1.0, ALU.add, ALU.mult)
 
-        y_sb = []
-        for t in range(PACK):
-            y_t = keep.tile([P, 2, PAIRS + PAD], F32, name=f"y{t}", tag=f"row{t}")
-            nc.gpsimd.memset(y_t[:, 0, PAIRS:], HIGHEST)
-            y_sb.append(y_t)
+        entries_of = [offsets[:, half * BANK // 16 : (half + 1) * BANK // 16] for half in range(2)]
+        picked_scales = []
+        for half in range(2):
+            scales = keep.tile([P, BANK], U8, name=f"picked_scales{half}", align_bytes=64)
+            nc.vector.tensor_copy(scales[:], table_scales[:].indirect(entries_of[half]))
+            picked_scales.append(scales)
 
-        def gather(half):
-            entries = offsets[:, half * BANK // 16 : (half + 1) * BANK // 16]
-            scales = keep.tile([P, BANK], U8, name=f"picked_scales{half}", tag=f"scales_slot{half}", align_bytes=64)
-            nc.vector.tensor_copy(scales[:], table_scales[:].indirect(entries))
-            words = keep.tile([P, BANK], U32, name=f"picked_words{half}", tag=f"words_slot{half}", align_bytes=64)
-            nc.vector.tensor_copy(words[:], table_words[:].bitcast(U32).indirect(entries))
-            return words, scales
-
-        picked = [gather(0)]
-
-        w1_bf = [
-            keep.tile([P, 2, P, PACK], BF16, name="w1_bf_low", tag="scales_slot1", align_bytes=64),
-            keep.tile([P, 2, P, PACK], BF16, name="w1_bf_high", tag="words_slot1", align_bytes=64),
-        ]
-        for pair in range(2):
-            dealt = w1_bf[pair][:].rearrange("p t m j -> p m t j")
-            ts = slice(2 * pair, 2 * pair + 2)
-            low = w1_raw[0][:].rearrange("p j (m t) -> p m t j", t=PACK)[:, :, ts]
-            high = w1_raw[1][:].rearrange("p j (m t) -> p m t j", t=PACK)[:, :, ts]
-            nc.scalar.copy(dealt[:, 0:64], low)
-            if pair == 0:
-                nc.vector.tensor_copy(dealt[:, 64:128], high)
-            else:
-                nc.scalar.copy(dealt[:, 64:128], high)
+        w1_bf = [keep.tile([P, 2, P, PACK], BF16, name=f"w1_bf{tile_pair}", align_bytes=64) for tile_pair in range(2)]
+        for half, raw in enumerate((w1_early, w1_late)):
+            units = slice(half * P // 2, (half + 1) * P // 2)
+            for tile_pair in range(2):
+                nc.scalar.copy(
+                    w1_bf[tile_pair][:].rearrange("p t m j -> p m t j")[:, units],
+                    raw[:].rearrange("p j (m t) -> p m t j", t=PACK)[:, :, 2 * tile_pair : 2 * tile_pair + 2],
+                )
         w1_codes = keep.tile([P, H], U32, name="w1_codes", align_bytes=64)
         w1_scales = keep.tile([P, H], U8, name="w1_scales", align_bytes=64)
         for t in range(PACK):
@@ -113,42 +98,64 @@ def tile_picked_ytonem_local_p_kernel(tc, x_words, x_scales, w1, unit, wo, skip,
                 in_=w1_bf[t // 2][:, t % 2].rearrange("p m j -> p (m j)"),
             )
 
-        first_sums = keep.tile([P, PACK], F32, name="first_sums")
-        second_sums = keep.tile([P, PACK], F32, name="second_sums")
-        half_bias = keep.tile([P, PACK], F32, name="half_bias")
-        exp_bias = keep.tile([P, PACK], F32, name="exp_bias")
-        picked.append(gather(1))
+        picked_words = []
         for half in range(2):
-            if True:
-                for t in range(PACK):
-                    cols = slice(t * P, (t + 1) * P)
-                    bank = psum.tile([P, BANK], F32, name=f"y_bank{t}{half}", tag=f"bank{2 * t + half}")
-                    nc.tensor.matmul_mx(
-                        out=bank[:],
-                        lhsT=w1_codes[:, cols].bitcast(FP8X4),
-                        lhsT_scale=w1_scales[:, cols],
-                        rhs=picked[half][0][:].bitcast(FP8X4),
-                        rhs_scale=picked[half][1][:],
-                        start=True,
-                        stop=True,
+            words = keep.tile([P, BANK], U32, name=f"picked_words{half}", tag=f"words{half}", align_bytes=64)
+            nc.vector.tensor_copy(words[:], table_words[:].bitcast(U32).indirect(entries_of[half]))
+            picked_words.append(words)
+
+        v_rows = [keep.tile([P, 2, PAIRS + PAD], F32, name="v0", tag="w1_late")]
+        nc.scalar.activation(
+            v_rows[0][:, 0, PAIRS:],
+            logs[:, 1:3, :].rearrange("p f t -> p (f t)"),
+            ACT.Exp,
+            bias=PAD_EXPONENT,
+            scale=0.0,
+        )
+        for t in range(1, PACK):
+            v_t = keep.tile([P, 2, PAIRS + PAD], F32, name=f"v{t}")
+            nc.scalar.copy(v_t[:, 0, PAIRS:], v_rows[0][:, 0, PAIRS:])
+            v_rows.append(v_t)
+
+        sums = keep.tile([P, 2, PACK], F32, name="sums")
+        exp_bias = keep.tile([P, PACK], F32, name="exp_bias")
+        for half in range(2):
+            for t in range(PACK):
+                cols = slice(t * P, (t + 1) * P)
+                bank = psum.tile([P, BANK], F32, name=f"y_bank{t}{half}", tag=f"bank{2 * t + half}")
+                nc.tensor.matmul_mx(
+                    out=bank[:],
+                    lhsT=w1_codes[:, cols].bitcast(FP8X4),
+                    lhsT_scale=w1_scales[:, cols],
+                    rhs=picked_words[half][:].bitcast(FP8X4),
+                    rhs_scale=picked_scales[half][:],
+                    start=True,
+                    stop=True,
+                )
+                v_part = v_rows[t][:, :, half * BANK // 2 : (half + 1) * BANK // 2]
+                by_parity = bank[:].rearrange("p (k two) -> p two k", two=2)
+                column = slice(t, t + 1)
+                if half == 0 or t < FIRST_VECTOR_TILE:
+                    nc.scalar.activation(v_part, by_parity, ACT.Copy, scale=-1.0 / S, accum_out=sums[:, half, column])
+                else:
+                    nc.vector.tensor_scalar(
+                        v_part, by_parity, -1.0 / S, 0.0, ALU.mult, ALU.add, accum_out=sums[:, half, column]
                     )
-                    planes = y_sb[t][:, :, half * BANK // 2 : (half + 1) * BANK // 2]
-                    by_parity = bank[:].rearrange("p (k two) -> p two k", two=2)
-                    if half == 0:
-                        nc.scalar.activation(planes, by_parity, ACT.Copy, scale=-1.0 / S, accum_out=first_sums[:, t : t + 1])
-                    elif t in VECTOR_TILES:
-                        nc.vector.tensor_scalar(
-                            planes, by_parity, -1.0 / S, half_bias[:, t : t + 1], ALU.mult, ALU.add, accum_out=exp_bias[:, t : t + 1]
-                        )
-                    else:
-                        nc.scalar.activation(planes, by_parity, ACT.Copy, scale=-1.0 / S, accum_out=second_sums[:, t : t + 1])
-                        nc.scalar.activation(
-                            exp_bias[:, t : t + 1], second_sums[:, t : t + 1], ACT.Identity, bias=half_bias[:, t : t + 1]
-                        )
-            if half == 0:
-                nc.vector.tensor_tensor(half_bias[:], first_sums[:], log_gain[:], ALU.add)
-        wo_raw = keep.tile([P, PACK, N], F32, name="wo_raw", tag="weights0")
-        nc.sync.dma_start(wo_raw[:], wo.rearrange("(p j) n -> p j n", j=PACK))
+                if half == 1:
+                    nc.vector.scalar_tensor_tensor(
+                        exp_bias[:, column], sums[:, 0, column], log_gain[:, column], sums[:, 1, column], ALU.add, ALU.add
+                    )
+
+        wo_bf = keep.tile([P, N, PACK], BF16, name="wo_bf", align_bytes=64)
+        for n0 in range(0, N, N // 4):
+            nc.gpsimd.tensor_tensor(
+                wo_bf[:, n0 : n0 + N // 4].rearrange("p (c i) j -> p c j i", i=2),
+                wo_raw[:, :, n0 : n0 + N // 4].rearrange("p j (c i) -> p c j i", i=2),
+                unit_sign[:].unsqueeze(1).unsqueeze(3).to_broadcast([P, N // 8, PACK, 2]),
+                ALU.mult,
+            )
+        wo_codes = keep.tile([P, N], U32, name="wo_codes", tag="words1", align_bytes=64)
+        wo_scales = keep.tile([P, N], U8, name="wo_scales", align_bytes=64)
         skip_sb = keep.tile([P, 2, S], F32, name="skip_sb", tag="table", align_bytes=64)
         for mt in range(2):
             nc.sync.dma_start(skip_sb[:, mt, :], skip[mt * P : (mt + 1) * P, :])
@@ -158,45 +165,49 @@ def tile_picked_ytonem_local_p_kernel(tc, x_words, x_scales, w1, unit, wo, skip,
 
         numerator = keep.tile([P, PACK, 2, PAIRS], F32, name="numerator")
         for t in range(PACK):
-            nc.scalar.activation(numerator[:, t], y_sb[t][:, :, 0:PAIRS], ACT.Exp, bias=exp_bias[:, t : t + 1], scale=-float(S))
-
-        pair_max = []
-        for t in range(PACK):
-            pair_t = keep.tile([P, PAIRS], F32, name=f"pair_max{t}")
-            pair_max.append(pair_t)
-        largest = []
-        for t in range(PACK):
-            largest_t = keep.tile([P, 2, PAIRS], F32, name=f"largest{t}")
-            largest.append(largest_t)
-
-        def pair_step(t):
-            nc.vector.tensor_tensor(pair_max[t][:], y_sb[t][:, 0, 0:PAIRS], y_sb[t][:, 1, 0:PAIRS], ALU.min)
-
-        def neighbour_step(t):
-            flat = y_sb[t][:].rearrange("p two k -> p (two k)")
-            reach = PAIRS + PAD - 2
-            outer = flat[:, 1 : 1 + 2 * reach].rearrange("p (two k) -> p two k", two=2)[:, :, 0:PAIRS]
-            nc.vector.tensor_tensor(
-                largest[t][:], pair_max[t][:].unsqueeze(1).to_broadcast([P, 2, PAIRS]), outer, ALU.min
+            nc.scalar.activation(
+                numerator[:, t], v_rows[t][:, :, 0:PAIRS], ACT.Exp, bias=exp_bias[:, t : t + 1], scale=-float(S)
             )
 
-        pair_step(0)
-        for t in range(PACK):
-            if t + 1 < PACK:
-                pair_step(t + 1)
-            neighbour_step(t)
+        pair_min = [keep.tile([P, PAIRS], F32, name=f"pair_min{t}") for t in range(PACK)]
+        smallest = [keep.tile([P, 2, PAIRS], F32, name=f"smallest{t}") for t in range(PACK)]
+
+        def pair_step(t, half):
+            ks = slice(half * PAIRS // 2, (half + 1) * PAIRS // 2)
+            nc.vector.tensor_tensor(pair_min[t][:, ks], v_rows[t][:, 0, ks], v_rows[t][:, 1, ks], ALU.min)
+
+        def neighbour_step(t, half):
+            ks = slice(0, SEAM) if half == 0 else slice(SEAM, PAIRS)
+            row = v_rows[t][:].rearrange("p two k -> p (two k)")
+            reach = PAIRS + PAD - 2
+            outer = row[:, 1 : 1 + 2 * reach].rearrange("p (two k) -> p two k", two=2)[:, :, ks]
+            nc.vector.tensor_tensor(
+                smallest[t][:, :, ks],
+                pair_min[t][:, ks].unsqueeze(1).to_broadcast([P, 2, ks.stop - ks.start]),
+                outer,
+                ALU.min,
+            )
+
+        def window_steps(half):
+            pair_step(0, half)
+            for t in range(PACK):
+                if t + 1 < PACK:
+                    pair_step(t + 1, half)
+                neighbour_step(t, half)
+
+        window_steps(0)
+        nc.vector.quantize_mx(
+            out=wo_codes[:].bitcast(FP8X4), scales=wo_scales[:], in_=wo_bf[:].rearrange("p n j -> p (n j)")
+        )
 
         out_rows = out.rearrange("(mt p) n -> p mt n", p=P)
-        first = 0
-        for c, pairs in enumerate(CHUNKS):
-            ks = slice(first, first + pairs)
-            entries = slice(2 * first, 2 * (first + pairs))
-            width = 2 * pairs
-            first = first + pairs
-            damping = keep.tile([P, PACK, 2, pairs], F32, name=f"damping{c}", tag=f"row{PACK - 1 - c}" if c < PACK else f"damping{c}")
+
+        def make_zz(c, ks):
+            pairs = ks.stop - ks.start
+            damping = keep.tile([P, PACK, 2, pairs], F32, name=f"damping{c}")
             for t in range(PACK):
                 nc.scalar.activation(
-                    damping[:, t], largest[t][:, :, ks], ACT.Sigmoid, bias=sigmoid_bias[:, t : t + 1], scale=float(S)
+                    damping[:, t], smallest[t][:, :, ks], ACT.Sigmoid, bias=sigmoid_bias[:, t : t + 1], scale=float(S)
                 )
             zz_bf = keep.tile([P, 2, pairs, PACK], BF16, name=f"zz_bf{c}", align_bytes=64)
             for parity in range(2):
@@ -206,24 +217,15 @@ def tile_picked_ytonem_local_p_kernel(tc, x_words, x_scales, w1, unit, wo, skip,
                     damping[:, :, 1 - parity, :].rearrange("p t (c i) -> p c t i", i=2),
                     ALU.mult,
                 )
+            return zz_bf
+
+        def read_out(c, ks, zz_bf):
+            width = 2 * (ks.stop - ks.start)
             zz_codes = keep.tile([P, width], U32, name=f"zz_codes{c}", align_bytes=64)
             zz_scales = keep.tile([P, width], U8, name=f"zz_scales{c}", align_bytes=64)
             nc.vector.quantize_mx(
                 out=zz_codes[:].bitcast(FP8X4), scales=zz_scales[:], in_=zz_bf[:].rearrange("p two k t -> p (two k t)")
             )
-            if c == 0:
-                wo_bf = keep.tile([P, N, PACK], BF16, name="wo_bf", align_bytes=64)
-                nc.vector.tensor_tensor(
-                    wo_bf[:].rearrange("p (c i) j -> p c j i", i=2),
-                    wo_raw[:].rearrange("p j (c i) -> p c j i", i=2),
-                    unit_sign[:].unsqueeze(1).unsqueeze(3).to_broadcast([P, N // 2, PACK, 2]),
-                    ALU.mult,
-                )
-                wo_codes = keep.tile([P, N], U32, name="wo_codes", align_bytes=64)
-                wo_scales = keep.tile([P, N], U8, name="wo_scales", align_bytes=64)
-                nc.vector.quantize_mx(
-                    out=wo_codes[:].bitcast(FP8X4), scales=wo_scales[:], in_=wo_bf[:].rearrange("p n j -> p (n j)")
-                )
             readout = psum.tile([P, 2, width], F32, name=f"readout{c}", tag=f"bank{c}")
             for mt in range(2):
                 cols = slice(mt * P, (mt + 1) * P)
@@ -236,7 +238,11 @@ def tile_picked_ytonem_local_p_kernel(tc, x_words, x_scales, w1, unit, wo, skip,
                     start=True,
                     stop=True,
                 )
-            result = keep.tile([P, 2, width], F32, name=f"result{c}")
+            return readout
+
+        def finish(c, ks, readout):
+            entries = slice(2 * ks.start, 2 * ks.stop)
+            result = keep.tile([P, 2, entries.stop - entries.start], F32, name=f"result{c}")
             nc.vector.tensor_tensor(
                 result[:].rearrange("p mt (k two) -> p mt k two", two=2),
                 readout[:].rearrange("p mt (two k) -> p mt k two", two=2),
@@ -244,3 +250,16 @@ def tile_picked_ytonem_local_p_kernel(tc, x_words, x_scales, w1, unit, wo, skip,
                 ALU.add,
             )
             nc.sync.dma_start(out_rows[:, :, entries], result[:])
+
+        ranges = [slice(sum(CHUNKS[:c]), sum(CHUNKS[: c + 1])) for c in range(len(CHUNKS))]
+        last = len(CHUNKS) - 1
+        products, readouts = [], []
+        for c in range(last + 3):
+            if c <= last:
+                if ranges[c].start < SEAM < ranges[c].stop:
+                    window_steps(1)
+                products.append(make_zz(c, ranges[c]))
+            if 1 <= c <= last + 1:
+                readouts.append(read_out(c - 1, ranges[c - 1], products[c - 1]))
+            if c >= 2:
+                finish(c - 2, ranges[c - 2], readouts[c - 2])

import math
from contextlib import ExitStack

import concourse.mybir as mybir

H, K, T, S, N = 512, 512, 2048, 1024, 256
FLOPS = 2 * K * H * S + 2 * H * N * S

F32 = mybir.dt.float32
BF16 = mybir.dt.bfloat16
I32 = mybir.dt.int32
U32 = mybir.dt.uint32
U16 = mybir.dt.uint16
U8 = mybir.dt.uint8
FP8X4 = mybir.dt.float8_e4m3fn_x4
ALU = mybir.AluOpType
ACT = mybir.ActivationFunctionType

P = 128
PACK = 4
BANK = 512
PAIRS = S // 2
PAD = 8
PAD_EXPONENT = 88.0
LN_EDGE = 2.0**63
SEAM = PAIRS // 2 - 4
FIRST_VECTOR_TILE = 2
CHUNKS = (32, 64, 128, 128, 128, 32)


def tile_picked_ytonem_local_p_kernel(
    tc, x_words, x_scales, w1, unit, wo, skip, offs, out
):
    nc = tc.nc
    with ExitStack() as ctx:
        keep = ctx.enter_context(tc.tile_pool(name="keep", bufs=1))
        psum = ctx.enter_context(tc.psum_pool(name="psum", bufs=1))

        offsets = keep.tile([P, S // 16], U16, name="offsets")
        nc.sync.dma_start(offsets[:], offs)
        unit_sb = keep.tile([P, PACK], F32, name="unit_sb")
        nc.sync.dma_start(unit_sb[:], unit.rearrange("(p t) o -> p (t o)", t=PACK))

        w1_rows = w1.rearrange("(p j) c -> p j c", j=PACK)
        w1_early = keep.tile([P, PACK, H // 2], F32, name="w1_early")
        nc.sync.dma_start(w1_early[:], w1_rows[:, :, 0 : H // 2])
        table_scales = keep.tile([P, T], U8, name="table_scales", align_bytes=64)
        nc.vector.memset(table_scales[:].bitcast(I32), 0)
        for q in range(4):
            nc.sync.dma_start(
                table_scales[32 * q : 32 * q + 4, :].bitcast(I32), x_scales[0, 4 * q : 4 * q + 4, :].bitcast(I32)
            )
        w1_late = keep.tile([P, PACK, H // 2], F32, name="w1_late", tag="w1_late")
        nc.sync.dma_start(w1_late[:], w1_rows[:, :, H // 2 : H])
        table_words = keep.tile([P, T], I32, name="table_words", tag="table", align_bytes=64)
        nc.sync.dma_start(table_words[:], x_words[0].rearrange("p n t -> p (n t)").bitcast(I32))
        wo_raw = keep.tile([P, PACK, N], F32, name="wo_raw")
        nc.sync.dma_start(wo_raw[:], wo.rearrange("(p j) n -> p j n", j=PACK))

        magnitude = keep.tile([P, PACK], F32, name="magnitude")
        nc.vector.scalar_tensor_tensor(magnitude[:], unit_sb[:], -1.0, unit_sb[:], ALU.mult, ALU.max)
        factors = keep.tile([P, 3, PACK], F32, name="factors")
        nc.vector.tensor_scalar(factors[:, 0, :], magnitude[:], 1.0 / LN_EDGE, LN_EDGE, ALU.max, ALU.min)
        nc.vector.tensor_scalar(factors[:, 1, :], magnitude[:], LN_EDGE, 1.0 / LN_EDGE, ALU.max, ALU.mult)
        nc.vector.tensor_scalar(factors[:, 2, :], magnitude[:], 1.0 / LN_EDGE, LN_EDGE, ALU.min, ALU.mult)
        logs = keep.tile([P, 3, PACK], F32, name="logs")
        nc.scalar.activation(logs[:, 0:2, :], factors[:, 0:2, :], ACT.Ln)
        nc.scalar.activation(logs[:, 2, :], factors[:, 2, :], ACT.Ln, bias=0.5 / LN_EDGE, scale=0.8)
        log_gain = keep.tile([P, PACK], F32, name="log_gain")
        nc.vector.tensor_reduce(log_gain[:], logs[:].rearrange("p f t -> p t f"), mybir.AxisListType.X, ALU.add)
        twice_positive = keep.tile([P, PACK], F32, name="twice_positive")
        nc.gpsimd.tensor_scalar(twice_positive[:], unit_sb[:], 0.0, 2.0, ALU.is_ge, ALU.mult)
        unit_sign = keep.tile([P, PACK], F32, name="unit_sign")
        nc.gpsimd.tensor_scalar(unit_sign[:], twice_positive[:], -1.0, 1.0, ALU.add, ALU.mult)

        entries_of = [offsets[:, half * BANK // 16 : (half + 1) * BANK // 16] for half in range(2)]
        picked_scales = []
        for half in range(2):
            scales = keep.tile([P, BANK], U8, name=f"picked_scales{half}", align_bytes=64)
            nc.vector.tensor_copy(scales[:], table_scales[:].indirect(entries_of[half]))
            picked_scales.append(scales)

        w1_bf = [keep.tile([P, 2, P, PACK], BF16, name=f"w1_bf{tile_pair}", align_bytes=64) for tile_pair in range(2)]
        for half, raw in enumerate((w1_early, w1_late)):
            units = slice(half * P // 2, (half + 1) * P // 2)
            for tile_pair in range(2):
                nc.scalar.copy(
                    w1_bf[tile_pair][:].rearrange("p t m j -> p m t j")[:, units],
                    raw[:].rearrange("p j (m t) -> p m t j", t=PACK)[:, :, 2 * tile_pair : 2 * tile_pair + 2],
                )
        w1_codes = keep.tile([P, H], U32, name="w1_codes", align_bytes=64)
        w1_scales = keep.tile([P, H], U8, name="w1_scales", align_bytes=64)
        for t in range(PACK):
            cols = slice(t * P, (t + 1) * P)
            nc.vector.quantize_mx(
                out=w1_codes[:, cols].bitcast(FP8X4),
                scales=w1_scales[:, cols],
                in_=w1_bf[t // 2][:, t % 2].rearrange("p m j -> p (m j)"),
            )

        picked_words = []
        for half in range(2):
            words = keep.tile([P, BANK], U32, name=f"picked_words{half}", tag=f"words{half}", align_bytes=64)
            nc.vector.tensor_copy(words[:], table_words[:].bitcast(U32).indirect(entries_of[half]))
            picked_words.append(words)

        v_rows = [keep.tile([P, 2, PAIRS + PAD], F32, name="v0", tag="w1_late")]
        nc.scalar.activation(
            v_rows[0][:, 0, PAIRS:],
            logs[:, 1:3, :].rearrange("p f t -> p (f t)"),
            ACT.Exp,
            bias=PAD_EXPONENT,
            scale=0.0,
        )
        for t in range(1, PACK):
            v_t = keep.tile([P, 2, PAIRS + PAD], F32, name=f"v{t}")
            nc.scalar.copy(v_t[:, 0, PAIRS:], v_rows[0][:, 0, PAIRS:])
            v_rows.append(v_t)

        sums = keep.tile([P, 2, PACK], F32, name="sums")
        exp_bias = keep.tile([P, PACK], F32, name="exp_bias")
        for half in range(2):
            for t in range(PACK):
                cols = slice(t * P, (t + 1) * P)
                bank = psum.tile([P, BANK], F32, name=f"y_bank{t}{half}", tag=f"bank{2 * t + half}")
                nc.tensor.matmul_mx(
                    out=bank[:],
                    lhsT=w1_codes[:, cols].bitcast(FP8X4),
                    lhsT_scale=w1_scales[:, cols],
                    rhs=picked_words[half][:].bitcast(FP8X4),
                    rhs_scale=picked_scales[half][:],
                    start=True,
                    stop=True,
                )
                v_part = v_rows[t][:, :, half * BANK // 2 : (half + 1) * BANK // 2]
                by_parity = bank[:].rearrange("p (k two) -> p two k", two=2)
                column = slice(t, t + 1)
                if half == 0 or t < FIRST_VECTOR_TILE:
                    nc.scalar.activation(v_part, by_parity, ACT.Copy, scale=-1.0 / S, accum_out=sums[:, half, column])
                else:
                    nc.vector.tensor_scalar(
                        v_part, by_parity, -1.0 / S, 0.0, ALU.mult, ALU.add, accum_out=sums[:, half, column]
                    )
                if half == 1:
                    nc.vector.scalar_tensor_tensor(
                        exp_bias[:, column], sums[:, 0, column], log_gain[:, column], sums[:, 1, column], ALU.add, ALU.add
                    )

        wo_bf = keep.tile([P, N, PACK], BF16, name="wo_bf", align_bytes=64)
        for n0 in range(0, N, N // 4):
            nc.gpsimd.tensor_tensor(
                wo_bf[:, n0 : n0 + N // 4].rearrange("p (c i) j -> p c j i", i=2),
                wo_raw[:, :, n0 : n0 + N // 4].rearrange("p j (c i) -> p c j i", i=2),
                unit_sign[:].unsqueeze(1).unsqueeze(3).to_broadcast([P, N // 8, PACK, 2]),
                ALU.mult,
            )
        wo_codes = keep.tile([P, N], U32, name="wo_codes", tag="words1", align_bytes=64)
        wo_scales = keep.tile([P, N], U8, name="wo_scales", align_bytes=64)
        skip_sb = keep.tile([P, 2, S], F32, name="skip_sb", tag="table", align_bytes=64)
        for mt in range(2):
            nc.sync.dma_start(skip_sb[:, mt, :], skip[mt * P : (mt + 1) * P, :])

        sigmoid_bias = keep.tile([P, PACK], F32, name="sigmoid_bias")
        nc.vector.scalar_tensor_tensor(sigmoid_bias[:], log_gain[:], -math.log(0.8), exp_bias[:], ALU.add, ALU.subtract)

        numerator = keep.tile([P, PACK, 2, PAIRS], F32, name="numerator")
        for t in range(PACK):
            nc.scalar.activation(
                numerator[:, t], v_rows[t][:, :, 0:PAIRS], ACT.Exp, bias=exp_bias[:, t : t + 1], scale=-float(S)
            )

        pair_min = [keep.tile([P, PAIRS], F32, name=f"pair_min{t}") for t in range(PACK)]
        smallest = [keep.tile([P, 2, PAIRS], F32, name=f"smallest{t}") for t in range(PACK)]

        def pair_step(t, half):
            ks = slice(half * PAIRS // 2, (half + 1) * PAIRS // 2)
            nc.vector.tensor_tensor(pair_min[t][:, ks], v_rows[t][:, 0, ks], v_rows[t][:, 1, ks], ALU.min)

        def neighbour_step(t, half):
            ks = slice(0, SEAM) if half == 0 else slice(SEAM, PAIRS)
            row = v_rows[t][:].rearrange("p two k -> p (two k)")
            reach = PAIRS + PAD - 2
            outer = row[:, 1 : 1 + 2 * reach].rearrange("p (two k) -> p two k", two=2)[:, :, ks]
            nc.vector.tensor_tensor(
                smallest[t][:, :, ks],
                pair_min[t][:, ks].unsqueeze(1).to_broadcast([P, 2, ks.stop - ks.start]),
                outer,
                ALU.min,
            )

        def window_steps(half):
            pair_step(0, half)
            for t in range(PACK):
                if t + 1 < PACK:
                    pair_step(t + 1, half)
                neighbour_step(t, half)

        window_steps(0)
        nc.vector.quantize_mx(
            out=wo_codes[:].bitcast(FP8X4), scales=wo_scales[:], in_=wo_bf[:].rearrange("p n j -> p (n j)")
        )

        out_rows = out.rearrange("(mt p) n -> p mt n", p=P)

        def make_zz(c, ks):
            pairs = ks.stop - ks.start
            damping = keep.tile([P, PACK, 2, pairs], F32, name=f"damping{c}")
            for t in range(PACK):
                nc.scalar.activation(
                    damping[:, t], smallest[t][:, :, ks], ACT.Sigmoid, bias=sigmoid_bias[:, t : t + 1], scale=float(S)
                )
            zz_bf = keep.tile([P, 2, pairs, PACK], BF16, name=f"zz_bf{c}", align_bytes=64)
            for parity in range(2):
                nc.vector.tensor_tensor(
                    zz_bf[:, parity].rearrange("p (c i) t -> p c t i", i=2),
                    numerator[:, :, parity, ks].rearrange("p t (c i) -> p c t i", i=2),
                    damping[:, :, 1 - parity, :].rearrange("p t (c i) -> p c t i", i=2),
                    ALU.mult,
                )
            return zz_bf

        def read_out(c, ks, zz_bf):
            width = 2 * (ks.stop - ks.start)
            zz_codes = keep.tile([P, width], U32, name=f"zz_codes{c}", align_bytes=64)
            zz_scales = keep.tile([P, width], U8, name=f"zz_scales{c}", align_bytes=64)
            nc.vector.quantize_mx(
                out=zz_codes[:].bitcast(FP8X4), scales=zz_scales[:], in_=zz_bf[:].rearrange("p two k t -> p (two k t)")
            )
            readout = psum.tile([P, 2, width], F32, name=f"readout{c}", tag=f"bank{c}")
            for mt in range(2):
                cols = slice(mt * P, (mt + 1) * P)
                nc.tensor.matmul_mx(
                    out=readout[:, mt, :],
                    lhsT=wo_codes[:, cols].bitcast(FP8X4),
                    lhsT_scale=wo_scales[:, cols],
                    rhs=zz_codes[:].bitcast(FP8X4),
                    rhs_scale=zz_scales[:],
                    start=True,
                    stop=True,
                )
            return readout

        def finish(c, ks, readout):
            entries = slice(2 * ks.start, 2 * ks.stop)
            result = keep.tile([P, 2, entries.stop - entries.start], F32, name=f"result{c}")
            nc.vector.tensor_tensor(
                result[:].rearrange("p mt (k two) -> p mt k two", two=2),
                readout[:].rearrange("p mt (two k) -> p mt k two", two=2),
                skip_sb[:, :, entries].rearrange("p mt (k two) -> p mt k two", two=2),
                ALU.add,
            )
            nc.sync.dma_start(out_rows[:, :, entries], result[:])

        ranges = [slice(sum(CHUNKS[:c]), sum(CHUNKS[: c + 1])) for c in range(len(CHUNKS))]
        last = len(CHUNKS) - 1
        products, readouts = [], []
        for c in range(last + 3):
            if c <= last:
                if ranges[c].start < SEAM < ranges[c].stop:
                    window_steps(1)
                products.append(make_zz(c, ranges[c]))
            if 1 <= c <= last + 1:
                readouts.append(read_out(c - 1, ranges[c - 1], products[c - 1]))
            if c >= 2:
                finish(c - 2, ranges[c - 2], readouts[c - 2])
